import numpy as np
import ml_dtypes


def mxq(x, axis, fmt="e4m3"):
    dtype, down = {"e4m3": (ml_dtypes.float8_e4m3fn, 7), "e5m2": (ml_dtypes.float8_e5m2, 14)}[fmt]
    v = np.moveaxis(np.asarray(x, np.float32).astype(ml_dtypes.bfloat16).astype(np.float64), axis, -1)
    blocks = v.reshape(v.shape[:-1] + (-1, 32))
    amax = np.abs(blocks).max(-1, keepdims=True)
    byte = np.maximum(np.where(amax > 0, np.frexp(amax)[1] - 1 + 127, 0) - down, 1)
    scale = np.exp2(byte - 127.0)
    codes = (blocks / scale).astype(np.float32).astype(dtype).astype(np.float64)
    return np.moveaxis((codes * scale).reshape(v.shape), -1, axis)


WIDE = False


def mx_kscale(k):
    if not WIDE:
        return np.ones(k)
    levels = np.array([10, -10, 5, -5, 0])
    if k % 512:
        return np.exp2(np.random.permutation(np.resize(levels, k // 32))).repeat(32)
    a = np.empty((k // 512, 16))
    for p in range(k // 512):
        a[p, :8] = np.random.permutation(np.resize(levels, 8))
        for g in range(8):
            far = levels[np.abs(levels - a[p, g]) >= 10]
            a[p, g + 8] = far[np.random.randint(len(far))]
    return np.exp2(a.ravel()).repeat(32)


BF16 = ml_dtypes.bfloat16


def bf(x):
    return np.asarray(x, np.float32).astype(BF16)


def f64(x):
    return np.asarray(x).astype(np.float64)


E2M1 = np.array([0.0, 0.5, 1.0, 1.5, 2.0, 3.0, 4.0, 6.0, -0.0, -0.5, -1.0, -1.5, -2.0, -3.0, -4.0, -6.0])


def pack_weight(w, fmt):
    k, n = w.shape
    w = f64(bf(w)).reshape(k // 32, 32, n)
    amax = np.abs(w).max(1)
    if fmt == "e4m3":
        byte = np.frexp(amax)[1] - 1 + 127 - 7
    else:
        mant, ex = np.frexp(amax / 6.0)
        byte = np.where(mant > 0.5, ex, ex - 1) + 127
    byte = np.clip(np.where(amax > 0, byte, 1), 1, 254)
    scaled = (w * np.exp2(127.0 - byte)[:, None, :]).reshape(k, n).astype(np.float32)
    by_word = np.ascontiguousarray(scaled.reshape(k // 512, 128, 4, n).transpose(0, 1, 3, 2))
    if fmt == "e4m3":
        words = by_word.astype(ml_dtypes.float8_e4m3fn).view(np.uint8)
    else:
        c = by_word.astype(ml_dtypes.float4_e2m1fn).view(np.uint8) & 0xF
        words = c[..., 0::2] | (c[..., 1::2] << 4)
    return np.ascontiguousarray(words), np.ascontiguousarray(byte.astype(np.uint8).reshape(k // 512, 16, n))


def unpack_weight(words, scales, fmt):
    g, p, n, _ = words.shape
    if fmt == "e4m3":
        vals = np.ascontiguousarray(words).view(ml_dtypes.float8_e4m3fn).astype(np.float64)
    else:
        nib = np.empty((g, p, n, 4), np.uint8)
        nib[..., 0::2] = words & 0xF
        nib[..., 1::2] = words >> 4
        vals = E2M1[nib]
    vals = vals * np.repeat(np.exp2(scales.astype(np.float64) - 127.0), 8, axis=1)[..., None]
    return vals.transpose(0, 1, 3, 2).reshape(g * 512, n)
def pack4(w):
    words, scales = pack_weight(w, "e2m1")
    return words.reshape(words.shape[0], 128, -1), scales


def unpack4(words, scales):
    return unpack_weight(words.reshape(words.shape[0], 128, -1, 2), scales, "e2m1")


M, K, N, L = 1024, 1024, 1024, 1536

SHARP = 2.0


def sigmoid(x):
    return 0.5 * (1.0 + np.tanh(0.5 * x))


def relative_softmax(x, axis):
    e = np.exp(x - x.max(axis=axis, keepdims=True))
    return e / e.mean(axis=axis, keepdims=True)


def draw0():
    s, t = mx_kscale(K), mx_kscale(N)
    query = np.random.standard_normal((M, K)) * s
    w = np.random.standard_normal((K, N)) / np.sqrt(K) / s[:, None] * t
    u = np.random.standard_normal((K, N)) / np.sqrt(K) / s[:, None]
    w_words, w_scales = pack4(w)
    u_words, u_scales = pack4(u)
    return {"query": bf(query),
            "w_words": w_words, "w_scales": w_scales,
            "u_words": u_words, "u_scales": u_scales,
            "b": bf(0.3 * np.random.standard_normal(N) * t),
            "d": bf(0.5 * np.random.standard_normal(N)),
            "context": bf(2.0 * np.random.standard_normal((L, N)) / np.sqrt(N) / t),
            "row_bias": bf(0.3 * np.random.standard_normal(M)),
            "col_bias": bf(0.3 * np.random.standard_normal(L))}


def core(query, w_words, w_scales, u_words, u_scales, b, d, context, row_bias, col_bias):
    w = unpack4(w_words, w_scales)
    u = unpack4(u_words, u_scales)
    xq = mxq(f64(query), 1, "e4m3")
    value = (xq @ w) + f64(b)
    gate = sigmoid((xq @ u) + f64(d))
    h = value * gate
    z = mxq(h, 1, "e4m3") @ mxq(f64(context), 1, "e4m3").T
    a = np.tanh(z + f64(row_bias)[:, None] + f64(col_bias)[None, :])
    over_context = relative_softmax(SHARP * a, 1)
    over_query = relative_softmax(SHARP * a, 0)
    return over_context, over_query


def e4m3fn_bytes(y):
    return np.clip(np.asarray(y, np.float64), -448.0, 448.0).astype(np.float32).astype(ml_dtypes.float8_e4m3fn).view(np.uint8)


def e4m3fn_values(b):
    return np.asarray(b, np.uint8).view(ml_dtypes.float8_e4m3fn).astype(np.float64)


def setup_inputs():
    d = draw0()
    x0 = np.asarray(d['context']).astype(np.float64)
    s = (np.max(np.abs(x0), axis=(0,), keepdims=True) / 448.0).astype(np.float32)
    out = {}
    for k, v in d.items():
        if k == 'context':
            out['context_bytes'] = e4m3fn_bytes(x0 / s.astype(np.float64))
            out['context_scale'] = s
        else:
            out[k] = v
    return out


def reference(query, w_words, w_scales, u_words, u_scales, b, d, context_bytes, context_scale, row_bias, col_bias):
    return core(query, w_words, w_scales, u_words, u_scales, b, d, e4m3fn_values(context_bytes) * context_scale.astype(np.float64), row_bias, col_bias)

from contextlib import ExitStack
import concourse.mybir as mybir
from concourse.masks import make_identity
M, K, N, L = 1024, 1024, 1024, 1536
F32 = mybir.dt.float32
BF16 = mybir.dt.bfloat16
U32 = mybir.dt.uint32
I32 = mybir.dt.int32
U8 = mybir.dt.uint8
E4M3 = mybir.dt.float8_e4m3fn
FP8X4 = mybir.dt.float8_e4m3fn_x4
FP4X4 = mybir.dt.float4_e2m1fn_x4
ACT = mybir.ActivationFunctionType
ALU = mybir.AluOpType
AXX = mybir.AxisListType.X
P = 128
C = 512
KG = 2
MT = M // P
LC = L // C
HC_ENGINE = "ss"
CC_ENGINE = "svv"
ILV = "ssss"
HI_ENGINE = "ss"
GROUPS = [(0, 1), (2, 3), (4, 5), (6,), (7,)]
ROW_ENGINE = "ggggggvv"
MM_BUFS, TURN_BUFS, INV_BUFS = 4, 2, 1
ZT_BUFS, SIG_BUFS, COLRES_BUFS, WIDE_BUFS, CG_BUFS = 8, 3, 12, 4, 2

SEQ = """
l_w00 k_mean k_sraw l_q0 k_minus2 l_w01 k_ident l_q1 k_warm l_s13 l_s02 l_s00 k_table l_s01 pw001 l_s03 pw000 qt0 l_q2
qt1 pw011 l_w10 qc0 pw010 qc1 qt2 l_w11 l_b l_s11 l_s10 qt3 l_q3 qc2 ps00 l_d qc3 ps01 qt4 l_s12 qq01 qt5 l_c1 qq00 qc4
l_rb l_c2 pw110 l_c0 qc5 mu1 l_csc pw100 mu0 pw111 qt6 l_cb hg1 ps10 qt7 qc6 ps11 mu2 qc7 pw101 mv0 hg0 qq11 mv1 hg2
ho0 mv2 ho1 mu3 ho2 mv3 hg3 qq10 mu4 ho3 mu5 hg4 cp01 mv4 hg5 mu6 ii001 ho4 mv5 cp00 mv6 hg6 mu7 ii000 ho5 mu8 ho6 mv7
cp02 hg7 mu9 hg8 ct010 ho7 mu10 hg9 cp10 mv8 cc010 mv10 hg10 ho8 mv9 ii101 ho10 mu11 ho9 mv11 hg11 cp03 mu12 ii100
ct000 ho11 mv12 hg12 cp11 ct011 cc000 mu13 cc011 ho12 ct001 hg13 hq00 ct100 cc001 mv13 cq01 ii010 mu14 cc100 mu15 ho13
mv14 cq00 hg14 mv15 hq10 hg15 ii011 ho14 zm00 ho15 ct110 zb00 zm01 ii111 cp13 zm02 zm03 ii110 zb01 cc110 zt01 cp12 zt00
ze01 hq11 ct111 hq01 cc111 zm05 zb03 zm04 ze00 zb02 ct101 zt03 zb04 ca001 zm06 zt02 cc101 zm07 ze03 cq11 zt04 cm00 cq10
ze02 zb05 ze04 zb06 zm12 ca011 zt05 zb07 zm11 zt06 cp20 zm13 ze05 zm10 cp21 zt07 cm01 ca021 ze06 zb11 ze07 ct200 zb10
cm02 zt11 cp23 zt10 ze11 cm03 zb12 ze10 cp22 zt12 cm04 ca101 ze12 cc200 ct201 zb13 k_identb ct210 cv0 cc201 zt13 cs0
cc210 ze13 cq20 ct211 ca111 co00 zm14 cc211 dc00 cm10 zb14 cq21 zt14 zm15 co03 zm20 ze14 zb15 dc03 zm22 zb20 zt15 zm21
co04 zt20 zm16 co05 ze15 dc04 cm11 zb21 dc05 ze20 ca121 zb22 zt21 zm17 ri0 co07 zt22 zm23 co01 rf0 ze21 dc07 ro0 zm27
zb16 ze22 dc01 cm12 zb17 zt16 ri2 zb23 zt17 rf2 zm25 dr0 ri1 co06 ze16 rf1 zm26 ro1 zb27 ze17 dc06 cm13 co02 zt23 zb25
zt27 dc02 cm14 ro2 zb26 dr1 ze23 zt25 zm24 cv1 ze27 ri3 ca211 cs1 dr2 zb24 ze25 zt24 cm24 rf3 ca201 co10 zt26 co11 ze24
dc10 cm21 co13 ze26 dc11 ca221 co17 dc13 cm23 co12 dc17 co16 ro3 dc12 co15 cm20 dc16 ri4 co14 dc15 rf4 ri6 cm22 dr3 ri5
dc14 rf5 ro4 cv2 cs2 ro5 dr4 co24 rf6 co21 dc24 co25 dc21 dr5 co20 co23 ri7 co27 dc23 dc25 rf7 dc20 co26 dc27 co22 dc26
ro7 dc22 ro6 dr6 dr7
"""
FLOPS = 2 * (2 * M * K * N) + 2 * M * N * L


def tile_gated_coattention_affinity_f1_kernel(
    tc, query, w_words, w_scales, u_words, u_scales, b, d, context_bytes, context_scale, row_bias, col_bias, out_0, out_1
):
    nc = tc.nc
    steps = {}
    with ExitStack() as ctx:
        keep = ctx.enter_context(tc.tile_pool(name="keep", bufs=1))
        work = ctx.enter_context(tc.tile_pool(name="work", bufs=2))
        psum = ctx.enter_context(tc.psum_pool(name="psum", bufs=1))
        ctx.enter_context(tc.manual_schedule())

        warm = keep.tile([P, 1], F32, name="warm")
        sraw = keep.tile([P, 4, N], U8, name="sraw", align_bytes=64)
        ident = keep.tile([P, P], F32, name="ident")
        identb = keep.tile([P, P], BF16, name="identb")
        mean = keep.tile([P, 2], F32, name="mean")
        minus2 = keep.tile([P, 1], F32, name="minus2")
        wraw = [[keep.tile([P, 2 * N], U8, name="wraw%d%d" % (x, g), tag="big%d" % (4 + 2 * x + g), align_bytes=64) for g in range(KG)] for x in range(2)]
        qraw = [keep.tile([P, 2, K], BF16, name="qraw%d" % i, tag="big%d" % i, align_bytes=64) for i in range(4)]
        cbytes = [keep.tile([P, 4, N], U8, name="cbytes%d" % c, align_bytes=64) for c in range(LC)]
        csc = keep.tile([P, N], F32, name="csc")
        bt = keep.tile([P, KG, 4], BF16, name="bt")
        dt = keep.tile([P, KG, 4], BF16, name="dt")
        rbt = keep.tile([P, MT], BF16, name="rbt")
        cbt = keep.tile([P, L], BF16, name="cbt")
        xcodes = keep.tile([P, 2, KG, C], U32, name="xcodes", align_bytes=64)
        xscales = keep.tile([P, 2, KG, C], U8, name="xscales", align_bytes=64)
        wp = keep.tile([P, 2, KG, 2, 4, 2 * P], U8, name="wp", align_bytes=64)
        sp = keep.tile([P, 2, KG, 2, 4, P], U8, name="sp", align_bytes=64)
        hcodes = keep.tile([P, 2, M], U32, name="hcodes", align_bytes=64)
        hscales = keep.tile([P, 2, M], U8, name="hscales", align_bytes=64)
        ccodes = [keep.tile([P, 2, C], U32, name="ccodes%d" % c, align_bytes=64) for c in range(LC)]
        cscales = [keep.tile([P, 2, C], U8, name="cscales%d" % c, align_bytes=64) for c in range(LC)]
        rs = keep.tile([P, MT, LC], F32, name="rs")
        rsum = keep.tile([P, MT], F32, name="rsum")
        rinv = keep.tile([P, MT], F32, name="rinv")
        rfac = keep.tile([P, MT, 8], F32, name="rfac")
        q_rows = query.rearrange("(p j) k -> p j k", j=MT)
        o1_rows = out_1.rearrange("(p j) l -> p j l", j=MT)
        o0_rows = out_0.rearrange("(p j) l -> p j l", j=MT)
        T = {}

        def step(name, fn):
            steps[name] = fn

        step("k_warm", lambda: nc.vector.memset(warm[:], 0.0))
        step("k_table", lambda: nc.scalar.activation(out=warm[:], in_=warm[:], func=ACT.Sigmoid))
        step("k_sraw", lambda: nc.vector.memset(sraw[:].rearrange("p x n -> p (x n)").bitcast(I32), 0))
        step("k_ident", lambda: make_identity(nc, ident[:]))
        step("k_identb", lambda: nc.gpsimd.tensor_copy(out=identb[:], in_=ident[:]))
        step("k_mean", lambda: nc.gpsimd.memset(mean[:], 1.0 / M))
        step("k_minus2", lambda: nc.gpsimd.memset(minus2[:], -2.0))
        for i in range(4):
            step("l_q%d" % i, lambda i=i: nc.sync.dma_start(out=qraw[i][:], in_=q_rows[:, 2 * i : 2 * i + 2, :]))
        for x, words in ((0, u_words), (1, w_words)):
            for g in range(KG):
                step("l_w%d%d" % (x, g), lambda x=x, g=g, words=words: nc.sync.dma_start(out=wraw[x][g][:].bitcast(I32), in_=words[g].bitcast(I32)))
        for x, scales in ((0, u_scales), (1, w_scales)):
            for q in range(4):
                step("l_s%d%d" % (x, q), lambda x=x, q=q, scales=scales: nc.sync.dma_start(
                    out=sraw[32 * q : 32 * q + 4, 2 * x : 2 * x + 2, :].bitcast(I32),
                    in_=scales[:, 4 * q : 4 * q + 4, :].rearrange("g r n -> r g n").bitcast(I32),
                ))
        step("l_b", lambda: nc.sync.dma_start(out=bt[:], in_=b.rearrange("(g p t) -> p g t", p=P, t=4)))
        step("l_d", lambda: nc.sync.dma_start(out=dt[:], in_=d.rearrange("(g p t) -> p g t", p=P, t=4)))
        step("l_csc", lambda: nc.sync.dma_start(out=csc[:], in_=context_scale.rearrange("o n -> (o n)").partition_broadcast(P)))
        for c in range(LC):
            step("l_c%d" % c, lambda c=c: nc.sync.dma_start(out=cbytes[c][:], in_=context_bytes[c * C : (c + 1) * C, :].rearrange("(j p) n -> p j n", p=P)))
        step("l_rb", lambda: nc.sync.dma_start(out=rbt[:], in_=row_bias.rearrange("(p j) -> p j", j=MT)))
        step("l_cb", lambda: nc.sync.dma_start(out=cbt[:], in_=col_bias.partition_broadcast(P)))

        def bank(name="mm"):
            t = psum.tile([P, C], F32, name="mm", bufs=MM_BUFS)
            return t

        def turn_bank():
            t = psum.tile([P, 4, P], F32, name="turn", bufs=TURN_BUFS)
            return t

        def q_turn(mt):
            words = qraw[mt // 2][:, mt % 2, :].bitcast(F32)
            T["qt", mt] = turn_bank()
            for g in range(KG):
                for u in range(2):
                    nc.tensor.transpose(T["qt", mt][:, 2 * g + u, :], words[:, 256 * g + u : 256 * (g + 1) : 2], ident[:])

        def q_copy(mt):
            h, i = divmod(mt, 4)
            if ("xg", h) not in T:
                T["xg", h] = work.tile([P, KG * C * 4], BF16, name="xg", tag="wide", bufs=WIDE_BUFS, align_bytes=64)
            dst = T["xg", h][:].bitcast(F32).rearrange("p (g m u) -> p g m u", g=KG, u=2)[:, :, P * i : P * (i + 1), :]
            nc.scalar.copy(out=dst, in_=T["qt", mt][:].rearrange("p (g u) m -> p g m u", u=2))

        def q_quantize(h, g):
            nc.vector.quantize_mx(out=xcodes[:, h, g, :].bitcast(FP8X4), scales=xscales[:, h, g, :], in_=T["xg", h][:, g * 4 * C : (g + 1) * 4 * C])

        def permute_words(x, g, gn):
            src = wraw[x][g][:, gn * 1024 : (gn + 1) * 1024].rearrange("p (m t e) -> p t m e", t=4, e=2)
            nc.vector.tensor_copy(out=wp[:, x, g, gn, :, :].rearrange("p t (m e) -> p t m e", e=2), in_=src)

        def permute_scales(x, gn):
            src = sraw[:, 2 * x : 2 * x + 2, gn * C : (gn + 1) * C].rearrange("p g (m t) -> p g t m", t=4)
            nc.vector.tensor_copy(out=sp[:, x, :, gn, :, :], in_=src)

        def c_product(c, j):
            if ("cw", c) not in T:
                T["cw", c] = work.tile([P, 4, N], BF16, name="cwide", tag="wide", bufs=WIDE_BUFS, align_bytes=64)
            nc.vector.tensor_tensor(out=T["cw", c][:, j, :], in0=cbytes[c][:, j, :].bitcast(E4M3), in1=csc[:], op=ALU.mult)

        def c_turn(c, g, jp):
            T["ct", c, g, jp] = turn_bank()
            for u in range(2):
                for jj in range(2):
                    words = T["cw", c][:, 2 * jp + jj, :].bitcast(F32)
                    nc.tensor.transpose(T["ct", c, g, jp][:, 2 * u + jj, :], words[:, 256 * g + u : 256 * (g + 1) : 2], ident[:])

        def c_copy(c, g, jp):
            if ("cg", c, g) not in T:
                T["cg", c, g] = work.tile([P, 4 * C], BF16, name="cgroup", bufs=CG_BUFS, align_bytes=64)
            dst = T["cg", c, g][:].bitcast(F32).rearrange("p (l u) -> p l u", u=2)[:, 256 * jp : 256 * (jp + 1), :]
            eng = nc.scalar.copy if CC_ENGINE[c] == "s" else nc.vector.tensor_copy
            eng(out=dst, in_=T["ct", c, g, jp][:].rearrange("p (u j) l -> p (j l) u", u=2))

        def c_quantize(c, g):
            nc.vector.quantize_mx(out=ccodes[c][:, g, :].bitcast(FP8X4), scales=cscales[c][:, g, :], in_=T["cg", c, g][:])

        units = [(gn, h, t) for h in range(2) for gn in range(2) for t in range(4)]

        def project(k, x):
            gn, h, t = units[k]
            acc = bank()
            for g in range(KG):
                nc.tensor.matmul_mx(out=acc[:], lhsT=wp[:, x, g, gn, t, :].bitcast(FP4X4), lhsT_scale=sp[:, x, g, gn, t, :],
                    rhs=xcodes[:, h, g, :].bitcast(FP8X4), rhs_scale=xscales[:, h, g, :], start=(g == 0), stop=(g == KG - 1))
            T["uv", x, k] = acc

        def h_gate(k):
            gn, h, t = units[k]
            T["sig", k] = work.tile([P, C], F32, name="sig", bufs=SIG_BUFS)
            nc.scalar.activation(out=T["sig", k][:], in_=T["uv", 0, k][:], func=ACT.Sigmoid, bias=dt[:, gn, t : t + 1])

        def h_out(k):
            gn, h, t = units[k]
            if ("hp", gn, h) not in T:
                T["hp", gn, h] = work.tile([P, 4, C], BF16, name="hplanes", bufs=2, align_bytes=64)
            nc.vector.scalar_tensor_tensor(out=T["hp", gn, h][:, t, :], in0=T["uv", 1, k][:], scalar=bt[:, gn, t : t + 1], in1=T["sig", k][:], op0=ALU.add, op1=ALU.mult)

        def h_spread(gn, h, half):
            T["hs", gn, h, half] = psum.tile([P, 2 * C], BF16, name="hspread", tag="turn", bufs=TURN_BUFS)
            for i in range(2):
                m0 = 256 * half + 128 * i
                nc.tensor.matmul(T["hs", gn, h, half][:, C * i : C * (i + 1)], lhsT=identb[:], rhs=T["hp", gn, h][:, :, m0 : m0 + P].rearrange("p t m -> p m t"), start=True, stop=True)

        def h_interleave(gn, h, half):
            if ("hg", gn, h) not in T:
                T["hg", gn, h] = work.tile([P, 4 * C], BF16, name="hgroup", bufs=2, align_bytes=64)
            eng = nc.scalar.copy if HI_ENGINE[half] == "s" else nc.vector.tensor_copy
            eng(out=T["hg", gn, h][:, 2 * C * half : 2 * C * (half + 1)].rearrange("p (m t) -> p m t", t=4), in_=T["hp", gn, h][:, :, 256 * half : 256 * (half + 1)].rearrange("p t m -> p m t"))

        def h_collect(gn, h, half):
            if ("hg", gn, h) not in T:
                T["hg", gn, h] = work.tile([P, 4 * C], BF16, name="hgroup", bufs=2, align_bytes=64)
            eng = nc.scalar.copy if HC_ENGINE[half] == "s" else nc.vector.tensor_copy
            eng(out=T["hg", gn, h][:, 2 * C * half : 2 * C * (half + 1)], in_=T["hs", gn, h, half][:])

        def h_quantize(gn, h):
            cols = slice(h * C, (h + 1) * C)
            nc.vector.quantize_mx(out=hcodes[:, gn, cols].bitcast(FP8X4), scales=hscales[:, gn, cols], in_=T["hg", gn, h][:])

        for mt in range(MT):
            step("qt%d" % mt, lambda mt=mt: q_turn(mt))
            step("qc%d" % mt, lambda mt=mt: q_copy(mt))
        for x in range(2):
            for gn in range(2):
                for g in range(KG):
                    step("pw%d%d%d" % (x, g, gn), lambda x=x, g=g, gn=gn: permute_words(x, g, gn))
                step("ps%d%d" % (x, gn), lambda x=x, gn=gn: permute_scales(x, gn))
        for h in range(2):
            for g in range(KG):
                step("qq%d%d" % (h, g), lambda h=h, g=g: q_quantize(h, g))
        for k in range(16):
            step("mu%d" % k, lambda k=k: project(k, 0))
            step("mv%d" % k, lambda k=k: project(k, 1))
            step("hg%d" % k, lambda k=k: h_gate(k))
            step("ho%d" % k, lambda k=k: h_out(k))
            if k % 4 == 3:
                gn, h, t = units[k]
                if ILV[2 * h + gn] == "p":
                    for half in range(2):
                        step("is%d%d%d" % (gn, h, half), lambda gn=gn, h=h, half=half: h_spread(gn, h, half))
                        step("ic%d%d%d" % (gn, h, half), lambda gn=gn, h=h, half=half: h_collect(gn, h, half))
                else:
                    for half in range(2):
                        step("ii%d%d%d" % (gn, h, half), lambda gn=gn, h=h, half=half: h_interleave(gn, h, half))
                step("hq%d%d" % (gn, h), lambda gn=gn, h=h: h_quantize(gn, h))
        for c in range(LC):
            for j in range(4):
                step("cp%d%d" % (c, j), lambda c=c, j=j: c_product(c, j))
            for g in range(2):
                for jp in range(2):
                    step("ct%d%d%d" % (c, g, jp), lambda c=c, g=g, jp=jp: c_turn(c, g, jp))
                    step("cc%d%d%d" % (c, g, jp), lambda c=c, g=g, jp=jp: c_copy(c, g, jp))
                step("cq%d%d" % (c, g), lambda c=c, g=g: c_quantize(c, g))

        def exps(mt):
            if ("e", mt) not in T:
                T["e", mt] = keep.tile([P, L], F32, name="exps%d" % mt, tag="big%d" % mt, align_bytes=64)
            return T["e", mt]

        def z_mm(c, mt):
            acc = bank()
            for gn in range(2):
                nc.tensor.matmul_mx(out=acc[:], lhsT=hcodes[:, gn, P * mt : P * (mt + 1)].bitcast(FP8X4), lhsT_scale=hscales[:, gn, P * mt : P * (mt + 1)],
                    rhs=ccodes[c][:, gn, :].bitcast(FP8X4), rhs_scale=cscales[c][:, gn, :], start=(gn == 0), stop=(gn == 1))
            T["z", c, mt] = acc

        def z_bias(c, mt):
            T["zt", c, mt] = work.tile([P, C], F32, name="zt", bufs=ZT_BUFS)
            nc.vector.tensor_tensor(out=T["zt", c, mt][:], in0=T["z", c, mt][:], in1=cbt[:, c * C : (c + 1) * C], op=ALU.add)

        def z_tanh(c, mt):
            t = T["zt", c, mt]
            nc.scalar.activation(out=t[:], in_=t[:], func=ACT.Tanh, bias=rbt[:, mt : mt + 1])

        def z_exp(c, mt):
            nc.scalar.activation(out=exps(mt)[:, c * C : (c + 1) * C], in_=T["zt", c, mt][:], func=ACT.Exp, bias=minus2[:], scale=2.0, accum_out=rs[:, mt, c : c + 1])

        def col_add(c, q, k):
            cols = slice(c * C, (c + 1) * C)
            group = GROUPS[q]
            if k == 1:
                T["grp", c, q] = work.tile([P, C], F32, name="grp", bufs=3)
            first = exps(group[0])[:, cols] if k == 1 else T["grp", c, q][:]
            nc.gpsimd.tensor_tensor(out=T["grp", c, q][:], in0=first, in1=exps(group[k])[:, cols], op=ALU.add)

        sums_all = psum.tile([P, LC, len(GROUPS), 4, 2], F32, name="sums", bufs=1)

        def col_mm(c, q):
            group = GROUPS[q]
            src = T["grp", c, q][:] if len(group) > 1 else exps(group[0])[:, c * C : (c + 1) * C]
            for j in range(4):
                nc.tensor.matmul(sums_all[:, c, q, j, :], lhsT=src[:, P * j : P * (j + 1)], rhs=mean[:], start=True, stop=True)

        def col_vec(c):
            total = work.tile([P, 4], F32, name="total", bufs=2)
            nc.vector.tensor_reduce(out=total[:], in_=sums_all[:, c, :, :, 0].rearrange("p q j -> p j q"), axis=AXX, op=ALU.add)
            T["vec", c] = work.tile([P, 4], F32, name="vec", bufs=2)
            nc.vector.reciprocal(out=T["vec", c][:], in_=total[:])

        def col_spread(c):
            T["inv", c] = psum.tile([P, 4, P], F32, name="inv", bufs=INV_BUFS)
            for j in range(4):
                nc.tensor.matmul(T["inv", c][:, j, :], lhsT=T["vec", c][:, j : j + 1].to_broadcast([P, P]), rhs=ident[:], start=True, stop=True)

        def col_out(c, mt):
            cols = slice(c * C, (c + 1) * C)
            T["co", c, mt] = work.tile([P, C], F32, name="colres", bufs=COLRES_BUFS)
            nc.vector.tensor_tensor(out=T["co", c, mt][:], in0=exps(mt)[:, cols], in1=T["inv", c][:].rearrange("p j l -> p (j l)"), op=ALU.mult)

        def row_inv(mt):
            nc.vector.tensor_reduce(out=rsum[:, mt : mt + 1], in_=rs[:, mt, :], axis=AXX, op=ALU.add)
            nc.vector.reciprocal(out=rinv[:, mt : mt + 1], in_=rsum[:, mt : mt + 1])

        def row_fac(mt):
            nc.gpsimd.tensor_scalar(out=rfac[:, mt, 0:1], in0=rinv[:, mt : mt + 1], scalar1=float(L), scalar2=0.0, op0=ALU.mult, op1=ALU.add)

        def row_out(mt):
            engine = ROW_ENGINE[mt]
            T["ro", mt] = work.tile([P, L], F32, name="rowres", tag="wide", bufs=WIDE_BUFS, align_bytes=64)
            res = T["ro", mt]
            if engine == "g":
                nc.gpsimd.tensor_scalar(out=res[:], in0=exps(mt)[:], scalar1=rfac[:, mt, 0:1], scalar2=0.0, op0=ALU.mult, op1=ALU.add)
            elif engine == "v":
                nc.vector.tensor_scalar(out=res[:], in0=exps(mt)[:], scalar1=rfac[:, mt, 0:1], scalar2=None, op0=ALU.mult)
            else:
                nc.scalar.activation(out=res[:], in_=exps(mt)[:], func=ACT.Copy, scale=rfac[:, mt, 0:1])

        for half in range(2):
            for c in range(LC):
                for mt in range(4 * half, 4 * half + 4):
                    n = "%d%d" % (c, mt)
                    step("zm" + n, lambda c=c, mt=mt: z_mm(c, mt))
                    step("zb" + n, lambda c=c, mt=mt: z_bias(c, mt))
                    step("zt" + n, lambda c=c, mt=mt: z_tanh(c, mt))
                    step("ze" + n, lambda c=c, mt=mt: z_exp(c, mt))
        for c in range(LC):
            for q in range(len(GROUPS)):
                for k in range(1, len(GROUPS[q])):
                    step("ca%d%d%d" % (c, q, k), lambda c=c, q=q, k=k: col_add(c, q, k))
                step("cm%d%d" % (c, q), lambda c=c, q=q: col_mm(c, q))
            step("cv%d" % c, lambda c=c: col_vec(c))
            step("cs%d" % c, lambda c=c: col_spread(c))
            for mt in range(MT):
                n = "%d%d" % (c, mt)
                step("co" + n, lambda c=c, mt=mt: col_out(c, mt))
                step("dc" + n, lambda c=c, mt=mt: nc.sync.dma_start(out=o1_rows[:, mt, c * C : (c + 1) * C], in_=T["co", c, mt][:]))
        for mt in range(MT):
            step("ri%d" % mt, lambda mt=mt: row_inv(mt))
            step("rf%d" % mt, lambda mt=mt: row_fac(mt))
            step("ro%d" % mt, lambda mt=mt: row_out(mt))
            step("dr%d" % mt, lambda mt=mt: nc.sync.dma_start(out=o0_rows[:, mt, :], in_=T["ro", mt][:]))

        for name in SEQ.split():
            steps[name]()
